import numpy as np
import ml_dtypes


def mxq(x, axis, fmt="e4m3"):
    dtype, down = {"e4m3": (ml_dtypes.float8_e4m3fn, 7), "e5m2": (ml_dtypes.float8_e5m2, 14)}[fmt]
    v = np.moveaxis(np.asarray(x, np.float32).astype(ml_dtypes.bfloat16).astype(np.float64), axis, -1)
    blocks = v.reshape(v.shape[:-1] + (-1, 32))
    amax = np.abs(blocks).max(-1, keepdims=True)
    byte = np.maximum(np.where(amax > 0, np.frexp(amax)[1] - 1 + 127, 0) - down, 1)
    scale = np.exp2(byte - 127.0)
    codes = (blocks / scale).astype(np.float32).astype(dtype).astype(np.float64)
    return np.moveaxis((codes * scale).reshape(v.shape), -1, axis)


WIDE = False


def mx_kscale(k):
    if not WIDE:
        return np.ones(k)
    levels = np.array([10, -10, 5, -5, 0])
    if k % 512:
        return np.exp2(np.random.permutation(np.resize(levels, k // 32))).repeat(32)
    a = np.empty((k // 512, 16))
    for p in range(k // 512):
        a[p, :8] = np.random.permutation(np.resize(levels, 8))
        for g in range(8):
            far = levels[np.abs(levels - a[p, g]) >= 10]
            a[p, g + 8] = far[np.random.randint(len(far))]
    return np.exp2(a.ravel()).repeat(32)


def f64(x):
    return np.asarray(x).astype(np.float64)


def striped(idx):
    return np.tile(idx.reshape(-1, 16).T, (8, 1)).astype(np.uint16)


def unstriped(offs):
    return offs[:16].T.reshape(-1).astype(np.int64)


E2M1 = np.array([0.0, 0.5, 1.0, 1.5, 2.0, 3.0, 4.0, 6.0, -0.0, -0.5, -1.0, -1.5, -2.0, -3.0, -4.0, -6.0])


def pack_weight(w, fmt):
    k, n = w.shape
    w = f64(np.asarray(w, np.float32).astype(ml_dtypes.bfloat16)).reshape(k // 32, 32, n)
    amax = np.abs(w).max(1)
    if fmt == "e4m3":
        byte = np.frexp(amax)[1] - 1 + 127 - 7
    else:
        mant, ex = np.frexp(amax / 6.0)
        byte = np.where(mant > 0.5, ex, ex - 1) + 127
    byte = np.clip(np.where(amax > 0, byte, 1), 1, 254)
    scaled = (w * np.exp2(127.0 - byte)[:, None, :]).reshape(k, n).astype(np.float32)
    by_word = np.ascontiguousarray(scaled.reshape(k // 512, 128, 4, n).transpose(0, 1, 3, 2))
    if fmt == "e4m3":
        words = by_word.astype(ml_dtypes.float8_e4m3fn).view(np.uint8)
    else:
        c = by_word.astype(ml_dtypes.float4_e2m1fn).view(np.uint8) & 0xF
        words = (c[..., 0::2] | (c[..., 1::2] << 4)).reshape(k // 512, 128, 2 * n)
    return np.ascontiguousarray(words), np.ascontiguousarray(byte.astype(np.uint8).reshape(k // 512, 16, n))


def unpack_weight(words, scales, fmt):
    g, _, n = scales.shape
    words = np.ascontiguousarray(words).reshape(g, 128, n, -1)
    if fmt == "e4m3":
        vals = words.view(ml_dtypes.float8_e4m3fn).astype(np.float64)
    else:
        nib = np.empty((g, 128, n, 4), np.uint8)
        nib[..., 0::2] = words & 0xF
        nib[..., 1::2] = words >> 4
        vals = E2M1[nib]
    vals = vals * np.repeat(np.exp2(scales.astype(np.float64) - 127.0), 8, axis=1)[..., None]
    return vals.transpose(0, 1, 3, 2).reshape(g * 512, n)


def gelu(v):
    return 0.5 * v * (1.0 + np.tanh(np.sqrt(2.0 / np.pi) * (v + 0.044715 * v**3)))


def striped8(idx):
    return np.concatenate([v.reshape(-1, 16).T for v in idx]).astype(np.uint16)


def unstriped8(offs):
    return np.stack([offs[16 * g:16 * g + 16].T.reshape(-1) for g in range(8)]).astype(np.int64)


def heads(h, wgt, idx8):
    r = np.arange(h.shape[0])
    return wgt[r // 4 % 128] * h[r[:, None], idx8[r % 512 // 64]]


def put_heads(h, wgs, idx8, t2):
    r = np.arange(h.shape[0])
    page = np.zeros((h.shape[0], t2))
    page[r[:, None], idx8[r % 512 // 64]] = wgs[r // 4 % 128] * h
    return page


K, T, S, T2, P, H, N = 1024, 4096, 1024, 2048, 1024, 1024, 512

def setup_inputs():
    n = np.random.standard_normal
    s = mx_kscale(K)[:, None]
    u = mx_kscale(H)[:, None]
    d = {}
    d["tab_words"], d["tab_scales"] = pack_weight(n((K, T)) * s, "e4m3")
    d["offs"] = striped(np.random.permutation(T)[:S])
    d["offs2"] = striped8(np.stack([np.random.permutation(T2)[:S] for _ in range(8)]))
    d["offs3"] = striped8(np.stack([np.random.permutation(T2)[:P] for _ in range(8)]))
    d["w1"] = (n((K, H)) / (K ** 0.5 * s)).astype(np.float32)
    d["least"] = n((H, S)).astype(np.float32)
    d["gain"] = (np.exp(0.3 * n(H)) * u[:, 0]).astype(np.float32)
    d["wgs"] = np.repeat(np.random.uniform(0.5, 2.0, (8, S)), 16, axis=0).astype(np.float32)
    d["wgt"] = np.repeat(np.random.uniform(0.5, 2.0, (8, P)), 16, axis=0).astype(np.float32)
    d["market"] = (n((H, P)) * u).astype(np.float32)
    d["w2_words"], d["w2_scales"] = pack_weight(n((H, N)) / (H ** 0.5 * u), "e2m1")
    d["cap"] = (0.5 + n((N, P))).astype(np.float32)
    return d

def reference(tab_words, tab_scales, offs, offs2, offs3, w1, least, gain, wgs, wgt, market, w2_words, w2_scales, cap):
    v = unpack_weight(tab_words, tab_scales, "e4m3")[:, unstriped(offs)]
    sim = mxq(f64(w1), 0, "e4m3").T @ v
    h = f64(gain)[:, None] * np.maximum(sim, f64(least))
    page = put_heads(h, f64(wgs), unstriped8(offs2), T2)
    x = heads(page, f64(wgt), unstriped8(offs3))
    z = x + f64(market)
    w2 = unpack_weight(w2_words, w2_scales, "e2m1")
    y = w2.T @ mxq(z, 0, "e4m3")
    return np.minimum(y, f64(cap))

@@ -1,0 +1,309 @@
+from contextlib import ExitStack
+
+import concourse.mybir as mybir
+from concourse.masks import make_identity
+
+K, T, S, T2, M, H, N = 1024, 4096, 1024, 2048, 1024, 1024, 512
+FLOPS = 2 * K * H * S + 2 * H * N * M
+
+F32 = mybir.dt.float32
+BF16 = mybir.dt.bfloat16
+I32 = mybir.dt.int32
+U32 = mybir.dt.uint32
+U16 = mybir.dt.uint16
+U8 = mybir.dt.uint8
+FP8X4 = mybir.dt.float8_e4m3fn_x4
+FP4X4 = mybir.dt.float4_e2m1fn_x4
+ALU = mybir.AluOpType
+COPY = mybir.ActivationFunctionType.Copy
+
+P = 128
+HALF = 512
+CHUNKS = (256, 256, 256, 128, 128)
+
+
+def tile_list_opposition_docket_scores_kernel(
+    tc, tab_words, tab_scales, offs, offs2, offs3, w1, least, gain, wgs, wgt, market, w2_words, w2_scales, cap, out
+):
+    nc = tc.nc
+    with ExitStack() as ctx:
+        keep = ctx.enter_context(tc.tile_pool(name="keep", bufs=1))
+        ring = ctx.enter_context(tc.tile_pool(name="ring", bufs=1))
+        psum = ctx.enter_context(tc.psum_pool(name="psum", bufs=1))
+
+        def held(shape, dtype, name, tag=None):
+            return keep.tile(shape, dtype, name=name, tag=tag or name, align_bytes=64)
+
+        def turn(shape, dtype, tag, bufs):
+            return ring.tile(shape, dtype, name=tag, tag=tag, bufs=bufs, align_bytes=64)
+
+        tab_sc = held([P, T], U8, "tab_sc")
+        nc.vector.memset(tab_sc[:].bitcast(I32), 0)
+        pages = [held([P, T2], F32, f"page{i}") for i in range(4)]
+        w2_sc = held([P, 2, N], U8, "w2_sc")
+        ident = held([P, P], F32, "ident")
+
+        list1 = held([P, S // 16], U16, "list1")
+        list2 = held([P, S // 16], U16, "list2")
+        list3 = held([P, M // 16], U16, "list3")
+        nc.sync.dma_start(list1[:], offs)
+        nc.sync.dma_start(list2[:], offs2)
+        gain_sb = held([P, 2, 4], F32, "gain_sb")
+        nc.sync.dma_start(gain_sb[:], gain.rearrange("(b p i) -> p b i", b=2, i=4))
+        wgs_sb = [held([P, HALF], F32, f"wgs{h}") for h in range(2)]
+        nc.sync.dma_start(wgs_sb[0][:], wgs[:, 0:HALF])
+        tab = [held([P, T], I32, f"tab{a}", f"big{a}") for a in range(2)]
+        for a in range(2):
+            nc.sync.dma_start(tab[a][:], tab_words[a].rearrange("p t i -> p (t i)").bitcast(I32))
+        for q in range(4):
+            nc.scalar.dma_start(
+                tab_sc[32 * q : 32 * q + 8, :].bitcast(I32), tab_scales[:, 4 * q : 4 * q + 4, :].bitcast(I32)
+            )
+        nc.vector.memset(pages[0][:], 0.0)
+        nc.vector.memset(pages[1][:], 0.0)
+        nc.gpsimd.memset(pages[2][:], 0.0)
+        nc.gpsimd.memset(pages[3][:], 0.0)
+        nc.gpsimd.memset(w2_sc[:].rearrange("p a n -> p (a n)").bitcast(I32), 0)
+        make_identity(nc, ident[:])
+
+        least_rows = least.rearrange("(b p i) j -> b i p j", b=2, i=4)
+        least0 = [held([P, HALF], F32, f"least0_{h}") for h in range(2)]
+        least_sb = {}
+
+        def load_least(s):
+            least_sb[s] = held([P, S], F32, f"least{s}")
+            nc.sync.dma_start(least_sb[s][:], least_rows[s // 4, s % 4])
+
+        w1_raw = {}
+
+        def load_w1(a, b):
+            w1_raw[a, b] = held([P, 4, HALF], F32, f"w1_raw{a}{b}", f"w1_raw{a}")
+            nc.sync.dma_start(
+                w1_raw[a, b][:],
+                w1[HALF * a : HALF * (a + 1), HALF * b : HALF * (b + 1)].rearrange("(p j) c -> p j c", j=4),
+            )
+
+        nc.sync.dma_start(least0[0][:], least_rows[0, 0][:, 0:HALF])
+        load_w1(0, 0)
+        load_w1(1, 0)
+        nc.sync.dma_start(wgs_sb[1][:], wgs[:, HALF:S])
+        nc.sync.dma_start(least0[1][:], least_rows[0, 0][:, HALF:S])
+        load_least(1)
+        nc.sync.dma_start(list3[:], offs3)
+        wgt_sb = held([P, M], F32, "wgt_sb")
+        nc.sync.dma_start(wgt_sb[:], wgt)
+        load_least(2)
+        load_least(3)
+
+        v_sc = held([P, S], U8, "v_sc")
+        v_words = [held([P, S], U32, f"v_words{a}") for a in range(2)]
+        nc.vector.tensor_copy(v_sc[:], tab_sc[:].indirect(list1[:]))
+        for a in range(2):
+            nc.vector.tensor_copy(v_words[a][:], tab[a][:].bitcast(U32).indirect(list1[:]))
+
+        w1_codes = {(a, b): held([P, HALF], U32, f"w1_codes{a}{b}") for a in range(2) for b in range(2)}
+        w1_sc = {(a, b): held([P, HALF], U8, f"w1_sc{a}{b}") for a in range(2) for b in range(2)}
+
+        def round_w1(engine_copy, grouped, a, b, i0, i1):
+            engine_copy(
+                grouped[:].rearrange("p (i m j) -> p m j i", i=i1 - i0, j=4),
+                w1_raw[a, b][:].rearrange("p j (m i) -> p m j i", i=4)[:, :, :, i0:i1],
+            )
+
+        def quantise_w1(grouped, a, b, i0, i1, first):
+            cols = slice(P * i0, P * i1)
+            nc.vector.quantize_mx(
+                out=w1_codes[a, b][:, cols].bitcast(FP8X4),
+                scales=w1_sc[a, b][:, cols],
+                in_=grouped[:, HALF * (i0 - first) : HALF * (i1 - first)],
+            )
+
+        def similarity(s, h):
+            b, i = divmod(s, 4)
+            bank = psum.tile([P, HALF], F32, name="mx_bank", tag="mx_bank", bufs=4)
+            cols = slice(HALF * h, HALF * (h + 1))
+            for a in range(2):
+                nc.tensor.matmul_mx(
+                    out=bank[:],
+                    lhsT=w1_codes[a, b][:, P * i : P * (i + 1)].bitcast(FP8X4),
+                    lhsT_scale=w1_sc[a, b][:, P * i : P * (i + 1)],
+                    rhs=v_words[a][:, cols].bitcast(FP8X4),
+                    rhs_scale=v_sc[4 * a : P, cols],
+                    start=(a == 0),
+                    stop=(a == 1),
+                )
+            return bank
+
+        def row_gain(s):
+            return gain_sb[:, s // 4, s % 4 : s % 4 + 1]
+
+        wg0 = held([P, S], F32, "wg0", "slot_wg0")
+        nc.scalar.activation(wg0[:, 0:HALF], wgs_sb[0][:], COPY, scale=row_gain(0))
+        g00 = held([P, 4 * HALF], BF16, "g00", "slot_p")
+        round_w1(nc.scalar.copy, g00, 0, 0, 0, 4)
+        quantise_w1(g00, 0, 0, 0, 4, 0)
+        g10_first = held([P, HALF], BF16, "g10_first")
+        round_w1(nc.vector.tensor_copy, g10_first, 1, 0, 0, 1)
+        quantise_w1(g10_first, 1, 0, 0, 1, 0)
+        g10_rest = held([P, 3 * HALF], BF16, "g10_rest", "slot_q")
+        round_w1(nc.scalar.copy, g10_rest, 1, 0, 1, 4)
+        nc.scalar.activation(wg0[:, HALF:S], wgs_sb[1][:], COPY, scale=row_gain(0))
+        for h, slot in enumerate(("slot_h0", "slot_q")):
+            if h == 1:
+                quantise_w1(g10_rest, 1, 0, 1, 2, 1)
+                quantise_w1(g10_rest, 1, 0, 2, 4, 1)
+            bank = similarity(0, h)
+            floored = held([P, HALF], F32, f"floored0_{h}", slot)
+            nc.vector.tensor_tensor(floored[:], bank[:], least0[h][:], ALU.max)
+            nc.vector.tensor_tensor(
+                pages[0][:].indirect(list2[:, 32 * h : 32 * (h + 1)]),
+                floored[:],
+                wg0[:, HALF * h : HALF * (h + 1)],
+                ALU.mult,
+            )
+
+        load_w1(0, 1)
+        load_w1(1, 1)
+        for s in range(4, 8):
+            load_least(s)
+        market_sb = [held([P, 4, M], F32, f"market{b}", f"big{b}") for b in range(2)]
+        market_rows = market.rearrange("(b p i) m -> b p i m", b=2, i=4)
+        nc.sync.dma_start(market_sb[0][:], market_rows[0])
+        w2_sb = held([P, 2, 2 * N], U8, "w2_sb")
+        nc.sync.dma_start(w2_sb[:].bitcast(I32), w2_words.rearrange("a p c -> p a c").bitcast(I32))
+        for q in range(4):
+            nc.sync.dma_start(
+                w2_sc[32 * q : 32 * q + 4, :, :].bitcast(I32),
+                w2_scales[:, 4 * q : 4 * q + 4, :].rearrange("a r n -> r a n").bitcast(I32),
+            )
+        nc.sync.dma_start(market_sb[1][:], market_rows[1])
+
+        floored_of, weight_of, picked0 = {}, {}, {}
+
+        def weigh(s):
+            slot = "slot_q" if s == 3 else f"slot_wg{s % 2}"
+            weight_of[s] = held([P, S], F32, f"wg{s}", slot)
+            for h in range(2):
+                nc.scalar.activation(weight_of[s][:, HALF * h : HALF * (h + 1)], wgs_sb[h][:], COPY, scale=row_gain(s))
+
+        def floor(s):
+            floored_of[s] = held([P, S], F32, f"floored{s}", f"slot_h{s % 3}")
+            for h in range(2):
+                cols = slice(HALF * h, HALF * (h + 1))
+                bank = similarity(s, h)
+                nc.vector.tensor_tensor(floored_of[s][:, cols], bank[:], least_sb[s][:, cols], ALU.max)
+
+        def put(s):
+            nc.vector.tensor_tensor(pages[s % 4][:].indirect(list2[:]), floored_of[s][:], weight_of[s][:], ALU.mult)
+
+        def pick_whole(s):
+            picked0[s] = held([P, M], F32, f"picked{s}", f"least{s + 1}")
+            nc.vector.tensor_tensor(picked0[s][:], pages[s][:].indirect(list3[:]), wgt_sb[:], ALU.mult)
+
+        weigh(1)
+        floor(1)
+        pick_whole(0)
+        put(1)
+        weigh(2)
+        floor(2)
+        pick_whole(1)
+        put(2)
+        for a, slot in enumerate(("slot_p", "slot_q")):
+            grouped = held([P, 4 * HALF], BF16, f"g{a}1", slot)
+            round_w1(nc.scalar.copy, grouped, a, 1, 0, 4)
+            quantise_w1(grouped, a, 1, 0, 4, 0)
+        weigh(3)
+        floor(3)
+        pick_whole(2)
+        put(3)
+        weigh(4)
+        floor(4)
+        pick_whole(3)
+        for s in range(4, 7):
+            weigh(s + 1)
+            floor(s + 1)
+            put(s)
+        put(7)
+
+        def interleave(b, mb, picked_block, z_words):
+            cols = slice(P * mb, P * (mb + 1))
+            turned = psum.tile([P, 4, P], F32, name="turned", tag="turned", bufs=2)
+            for i in range(4):
+                nc.tensor.matmul(turned[:, i, :], lhsT=market_sb[b][:, i, cols], rhs=ident[:], is_transpose=True, start=True, stop=False)
+                nc.tensor.matmul(turned[:, i, :], lhsT=picked_block(i), rhs=ident[:], is_transpose=True, start=False, stop=True)
+            pairs = turn([P, 4 * P], BF16, "pairs", 3)
+            nc.scalar.copy(
+                pairs[:].rearrange("m (u p e) -> m u p e", u=2, e=2),
+                turned[:].rearrange("m (u e) p -> m u p e", u=2),
+            )
+            back = psum.tile([P, 2, P], F32, name="back", tag="back", bufs=2)
+            for u in range(2):
+                nc.tensor.transpose(back[:, u, :], pairs[:].bitcast(F32)[:, P * u : P * (u + 1)], ident[:])
+            nc.scalar.copy(z_words.rearrange("p (m u) -> p m u", u=2), back[:].rearrange("p u m -> p m u"))
+
+        z0_codes = held([P, M], U32, "z0_codes")
+        z0_sc = held([P, M], U8, "z0_sc")
+        for h in range(2):
+            z0 = held([P, 4 * HALF], BF16, f"z0_{h}")
+            for k in range(4):
+                mb = 4 * h + k
+                interleave(0, mb, lambda i: picked0[i][:, P * mb : P * (mb + 1)], z0[:].bitcast(F32)[:, 2 * P * k : 2 * P * (k + 1)])
+            cols = slice(HALF * h, HALF * (h + 1))
+            nc.vector.quantize_mx(out=z0_codes[:, cols].bitcast(FP8X4), scales=z0_sc[:, cols], in_=z0[:])
+
+        cap_sb = held([P, 4, M], F32, "cap_sb", "big0")
+        nc.sync.dma_start(cap_sb[:], cap.rearrange("(nb p) m -> p nb m", p=P))
+        out_rows = out.rearrange("(nb p) m -> p nb m", p=P)
+
+        def scores_pass(bank, b, codes, scales):
+            for nb in range(4):
+                nc.tensor.matmul_mx(
+                    out=bank[:, nb, :],
+                    lhsT=w2_sb[:, b, 2 * P * nb : 2 * P * (nb + 1)].bitcast(FP4X4),
+                    lhsT_scale=w2_sc[:, b, P * nb : P * (nb + 1)],
+                    rhs=codes.bitcast(FP8X4),
+                    rhs_scale=scales,
+                    start=(b == 0 and nb == 0),
+                    stop=(b == 1 and nb == 3),
+                )
+
+        chunk_slots = ("slot_wg0", "slot_h0", "slot_wg1", "slot_h1", "slot_wg0")
+        picked1 = {}
+
+        def pick_chunk(c):
+            m0, width = sum(CHUNKS[:c]), CHUNKS[c]
+            chunk = held([P, 4, width], F32, f"picked1_{c}", chunk_slots[c])
+            for i in range(4):
+                nc.vector.tensor_tensor(
+                    chunk[:, i, :],
+                    pages[i][:].indirect(list3[:, m0 // 16 : (m0 + width) // 16]),
+                    wgt_sb[:, m0 : m0 + width],
+                    ALU.mult,
+                )
+            for k in range(width // P):
+                picked1[m0 // P + k] = (chunk, k)
+
+        def finish(mb):
+            chunk, k = picked1[mb]
+            cols = slice(P * mb, P * (mb + 1))
+            bank = psum.tile([P, 4, P], F32, name="mx_bank", tag="mx_bank", bufs=4)
+            scores_pass(bank, 0, z0_codes[:, cols], z0_sc[:, cols])
+            z1 = turn([P, 4 * P], BF16, "z1", 3)
+            interleave(1, mb, lambda i: chunk[:, i, P * k : P * (k + 1)], z1[:].bitcast(F32))
+            codes = turn([P, P], U32, "z1_codes", 3)
+            scales = turn([P, P], U8, "z1_sc", 3)
+            nc.vector.quantize_mx(out=codes[:].bitcast(FP8X4), scales=scales[:], in_=z1[:])
+            scores_pass(bank, 1, codes[:], scales[:])
+            result = turn([P, 4, P], F32, "result", 4)
+            nc.vector.tensor_tensor(result[:], bank[:], cap_sb[:, :, cols], ALU.min)
+            nc.sync.dma_start(out_rows[:, :, cols], result[:])
+
+        pick_chunk(0)
+        done = 0
+        for c in range(1, len(CHUNKS) + 1):
+            if c < len(CHUNKS):
+                pick_chunk(c)
+            upto = sum(CHUNKS[:c]) // P
+            for mb in range(done, upto):
+                finish(mb)
+            done = upto

@@ -20,6 +20,7 @@ COPY = mybir.ActivationFunctionType.Copy
 P = 128
 HALF = 512
 CHUNKS = (256, 256, 256, 128, 128)
+WEIGHT_SLOTS = ("slot_wg0", "slot_wg1", "slot_wg0", "slot_q", "slot_wg1", "slot_wg0", "slot_q", "z0_1")
 
 
 def tile_list_opposition_docket_scores_kernel(
@@ -51,10 +52,12 @@ def tile_list_opposition_docket_scores_kernel(
         gain_sb = held([P, 2, 4], F32, "gain_sb")
         nc.sync.dma_start(gain_sb[:], gain.rearrange("(b p i) -> p b i", b=2, i=4))
         wgs_sb = [held([P, HALF], F32, f"wgs{h}") for h in range(2)]
-        nc.sync.dma_start(wgs_sb[0][:], wgs[:, 0:HALF])
         tab = [held([P, T], I32, f"tab{a}", f"big{a}") for a in range(2)]
-        for a in range(2):
+
+        def load_tab(a):
             nc.sync.dma_start(tab[a][:], tab_words[a].rearrange("p t i -> p (t i)").bitcast(I32))
+
+        load_tab(0)
         for q in range(4):
             nc.scalar.dma_start(
                 tab_sc[32 * q : 32 * q + 8, :].bitcast(I32), tab_scales[:, 4 * q : 4 * q + 4, :].bitcast(I32)
@@ -67,12 +70,22 @@ def tile_list_opposition_docket_scores_kernel(
         make_identity(nc, ident[:])
 
         least_rows = least.rearrange("(b p i) j -> b i p j", b=2, i=4)
-        least0 = [held([P, HALF], F32, f"least0_{h}") for h in range(2)]
         least_sb = {}
 
+        def load_least_half(s, h):
+            half = held([P, HALF], F32, f"least{s}_{h}")
+            nc.sync.dma_start(half[:], least_rows[s // 4, s % 4][:, HALF * h : HALF * (h + 1)])
+            least_sb[s, h] = half[:]
+
         def load_least(s):
-            least_sb[s] = held([P, S], F32, f"least{s}")
-            nc.sync.dma_start(least_sb[s][:], least_rows[s // 4, s % 4])
+            if s <= 4:
+                for h in range(2):
+                    load_least_half(s, h)
+            else:
+                whole = held([P, S], F32, f"least{s}")
+                nc.sync.dma_start(whole[:], least_rows[s // 4, s % 4])
+                for h in range(2):
+                    least_sb[s, h] = whole[:, HALF * h : HALF * (h + 1)]
 
         w1_raw = {}
 
@@ -83,11 +96,13 @@ def tile_list_opposition_docket_scores_kernel(
                 w1[HALF * a : HALF * (a + 1), HALF * b : HALF * (b + 1)].rearrange("(p j) c -> p j c", j=4),
             )
 
-        nc.sync.dma_start(least0[0][:], least_rows[0, 0][:, 0:HALF])
         load_w1(0, 0)
+        load_tab(1)
         load_w1(1, 0)
+        load_least_half(0, 0)
+        nc.sync.dma_start(wgs_sb[0][:], wgs[:, 0:HALF])
         nc.sync.dma_start(wgs_sb[1][:], wgs[:, HALF:S])
-        nc.sync.dma_start(least0[1][:], least_rows[0, 0][:, HALF:S])
+        load_least_half(0, 1)
         load_least(1)
         nc.sync.dma_start(list3[:], offs3)
         wgt_sb = held([P, M], F32, "wgt_sb")
@@ -118,10 +133,10 @@ def tile_list_opposition_docket_scores_kernel(
                 in_=grouped[:, HALF * (i0 - first) : HALF * (i1 - first)],
             )
 
-        def similarity(s, h):
+        def similarity(s, j0, width):
             b, i = divmod(s, 4)
-            bank = psum.tile([P, HALF], F32, name="mx_bank", tag="mx_bank", bufs=4)
-            cols = slice(HALF * h, HALF * (h + 1))
+            bank = psum.tile([P, width], F32, name="mx_bank", tag="mx_bank", bufs=4)
+            cols = slice(j0, j0 + width)
             for a in range(2):
                 nc.tensor.matmul_mx(
                     out=bank[:],
@@ -138,27 +153,28 @@ def tile_list_opposition_docket_scores_kernel(
             return gain_sb[:, s // 4, s % 4 : s % 4 + 1]
 
         wg0 = held([P, S], F32, "wg0", "slot_wg0")
-        nc.scalar.activation(wg0[:, 0:HALF], wgs_sb[0][:], COPY, scale=row_gain(0))
         g00 = held([P, 4 * HALF], BF16, "g00", "slot_p")
         round_w1(nc.scalar.copy, g00, 0, 0, 0, 4)
         quantise_w1(g00, 0, 0, 0, 4, 0)
         g10_first = held([P, HALF], BF16, "g10_first")
         round_w1(nc.vector.tensor_copy, g10_first, 1, 0, 0, 1)
         quantise_w1(g10_first, 1, 0, 0, 1, 0)
+        nc.scalar.activation(wg0[:, 0:HALF], wgs_sb[0][:], COPY, scale=row_gain(0))
         g10_rest = held([P, 3 * HALF], BF16, "g10_rest", "slot_q")
         round_w1(nc.scalar.copy, g10_rest, 1, 0, 1, 4)
         nc.scalar.activation(wg0[:, HALF:S], wgs_sb[1][:], COPY, scale=row_gain(0))
-        for h, slot in enumerate(("slot_h0", "slot_q")):
-            if h == 1:
+        for j0, width, slot in ((0, 256, "slot_h0"), (256, 256, "slot_h2"), (HALF, HALF, "slot_q")):
+            if j0 == HALF:
                 quantise_w1(g10_rest, 1, 0, 1, 2, 1)
                 quantise_w1(g10_rest, 1, 0, 2, 4, 1)
-            bank = similarity(0, h)
-            floored = held([P, HALF], F32, f"floored0_{h}", slot)
-            nc.vector.tensor_tensor(floored[:], bank[:], least0[h][:], ALU.max)
+            bank = similarity(0, j0, width)
+            floored = held([P, width], F32, f"floored0_{j0}", slot)
+            c0 = j0 % HALF
+            nc.vector.tensor_tensor(floored[:], bank[:], least_sb[0, j0 // HALF][:, c0 : c0 + width], ALU.max)
             nc.vector.tensor_tensor(
-                pages[0][:].indirect(list2[:, 32 * h : 32 * (h + 1)]),
+                pages[0][:].indirect(list2[:, j0 // 16 : (j0 + width) // 16]),
                 floored[:],
-                wg0[:, HALF * h : HALF * (h + 1)],
+                wg0[:, j0 : j0 + width],
                 ALU.mult,
             )
 
@@ -181,7 +197,7 @@ def tile_list_opposition_docket_scores_kernel(
         floored_of, weight_of, picked0 = {}, {}, {}
 
         def weigh(s):
-            slot = "slot_q" if s == 3 else f"slot_wg{s % 2}"
+            slot = WEIGHT_SLOTS[s]
             weight_of[s] = held([P, S], F32, f"wg{s}", slot)
             for h in range(2):
                 nc.scalar.activation(weight_of[s][:, HALF * h : HALF * (h + 1)], wgs_sb[h][:], COPY, scale=row_gain(s))
@@ -190,14 +206,14 @@ def tile_list_opposition_docket_scores_kernel(
             floored_of[s] = held([P, S], F32, f"floored{s}", f"slot_h{s % 3}")
             for h in range(2):
                 cols = slice(HALF * h, HALF * (h + 1))
-                bank = similarity(s, h)
-                nc.vector.tensor_tensor(floored_of[s][:, cols], bank[:], least_sb[s][:, cols], ALU.max)
+                bank = similarity(s, HALF * h, HALF)
+                nc.vector.tensor_tensor(floored_of[s][:, cols], bank[:], least_sb[s, h], ALU.max)
 
         def put(s):
             nc.vector.tensor_tensor(pages[s % 4][:].indirect(list2[:]), floored_of[s][:], weight_of[s][:], ALU.mult)
 
         def pick_whole(s):
-            picked0[s] = held([P, M], F32, f"picked{s}", f"least{s + 1}")
+            picked0[s] = held([P, M], F32, f"picked{s}", f"least{s + 1}_0")
             nc.vector.tensor_tensor(picked0[s][:], pages[s][:].indirect(list3[:]), wgt_sb[:], ALU.mult)
 
         weigh(1)
@@ -220,17 +236,18 @@ def tile_list_opposition_docket_scores_kernel(
         floor(4)
         pick_whole(3)
         for s in range(4, 7):
-            weigh(s + 1)
+            if s < 6:
+                weigh(s + 1)
             floor(s + 1)
             put(s)
-        put(7)
 
         def interleave(b, mb, picked_block, z_words):
             cols = slice(P * mb, P * (mb + 1))
             turned = psum.tile([P, 4, P], F32, name="turned", tag="turned", bufs=2)
             for i in range(4):
-                nc.tensor.matmul(turned[:, i, :], lhsT=market_sb[b][:, i, cols], rhs=ident[:], is_transpose=True, start=True, stop=False)
-                nc.tensor.matmul(turned[:, i, :], lhsT=picked_block(i), rhs=ident[:], is_transpose=True, start=False, stop=True)
+                nc.tensor.matmul(turned[:, i, :], lhsT=market_sb[b][:, i, cols], rhs=ident[:], is_transpose=True, start=(i == 0), stop=False)
+            for i in range(4):
+                nc.tensor.matmul(turned[:, i, :], lhsT=picked_block(i), rhs=ident[:], is_transpose=True, start=False, stop=(i == 3))
             pairs = turn([P, 4 * P], BF16, "pairs", 3)
             nc.scalar.copy(
                 pairs[:].rearrange("m (u p e) -> m u p e", u=2, e=2),
@@ -251,8 +268,13 @@ def tile_list_opposition_docket_scores_kernel(
             cols = slice(HALF * h, HALF * (h + 1))
             nc.vector.quantize_mx(out=z0_codes[:, cols].bitcast(FP8X4), scales=z0_sc[:, cols], in_=z0[:])
 
-        cap_sb = held([P, 4, M], F32, "cap_sb", "big0")
-        nc.sync.dma_start(cap_sb[:], cap.rearrange("(nb p) m -> p nb m", p=P))
+        weigh(7)
+        put(7)
+
+        cap_rows = cap.rearrange("(nb p) m -> p nb m", p=P)
+        cap_sb = [held([P, 4, HALF], F32, f"cap{h}", f"w1_raw{h}") for h in range(2)]
+        for h in range(2):
+            nc.sync.dma_start(cap_sb[h][:], cap_rows[:, :, HALF * h : HALF * (h + 1)])
         out_rows = out.rearrange("(nb p) m -> p nb m", p=P)
 
         def scores_pass(bank, b, codes, scales):
@@ -267,8 +289,8 @@ def tile_list_opposition_docket_scores_kernel(
                     stop=(b == 1 and nb == 3),
                 )
 
-        chunk_slots = ("slot_wg0", "slot_h0", "slot_wg1", "slot_h1", "slot_wg0")
-        picked1 = {}
+        chunk_slots = ("slot_h1", "z0_1", "z1_0", "z1_2", "z1_4")
+        blocks1 = {}
 
         def pick_chunk(c):
             m0, width = sum(CHUNKS[:c]), CHUNKS[c]
@@ -281,29 +303,36 @@ def tile_list_opposition_docket_scores_kernel(
                     ALU.mult,
                 )
             for k in range(width // P):
-                picked1[m0 // P + k] = (chunk, k)
+                blocks1[m0 // P + k] = (chunk, k)
 
-        def finish(mb):
-            chunk, k = picked1[mb]
+        open_banks = {}
+
+        def second_pass(mb):
+            chunk, k = blocks1[mb]
             cols = slice(P * mb, P * (mb + 1))
             bank = psum.tile([P, 4, P], F32, name="mx_bank", tag="mx_bank", bufs=4)
             scores_pass(bank, 0, z0_codes[:, cols], z0_sc[:, cols])
-            z1 = turn([P, 4 * P], BF16, "z1", 3)
+            z1 = held([P, 4 * P], BF16, f"z1_{mb}")
             interleave(1, mb, lambda i: chunk[:, i, P * k : P * (k + 1)], z1[:].bitcast(F32))
             codes = turn([P, P], U32, "z1_codes", 3)
             scales = turn([P, P], U8, "z1_sc", 3)
             nc.vector.quantize_mx(out=codes[:].bitcast(FP8X4), scales=scales[:], in_=z1[:])
             scores_pass(bank, 1, codes[:], scales[:])
+            open_banks[mb] = bank
+
+        def finish(mb):
+            cols = slice(P * mb, P * (mb + 1))
+            bank = open_banks[mb]
             result = turn([P, 4, P], F32, "result", 4)
-            nc.vector.tensor_tensor(result[:], bank[:], cap_sb[:, :, cols], ALU.min)
+            nc.vector.tensor_tensor(result[:], bank[:], cap_sb[mb // 4][:, :, P * (mb % 4) : P * (mb % 4 + 1)], ALU.min)
             nc.sync.dma_start(out_rows[:, :, cols], result[:])
 
         pick_chunk(0)
-        done = 0
-        for c in range(1, len(CHUNKS) + 1):
-            if c < len(CHUNKS):
-                pick_chunk(c)
-            upto = sum(CHUNKS[:c]) // P
-            for mb in range(done, upto):
-                finish(mb)
-            done = upto
+        pick_chunk(1)
+        for pair in range(4):
+            second_pass(2 * pair)
+            second_pass(2 * pair + 1)
+            if pair + 2 < len(CHUNKS):
+                pick_chunk(pair + 2)
+            finish(2 * pair)
+            finish(2 * pair + 1)

@@ -62,10 +62,8 @@ def tile_list_opposition_docket_scores_kernel(
             nc.scalar.dma_start(
                 tab_sc[32 * q : 32 * q + 8, :].bitcast(I32), tab_scales[:, 4 * q : 4 * q + 4, :].bitcast(I32)
             )
-        nc.vector.memset(pages[0][:], 0.0)
-        nc.vector.memset(pages[1][:], 0.0)
-        nc.gpsimd.memset(pages[2][:], 0.0)
-        nc.gpsimd.memset(pages[3][:], 0.0)
+        for page in pages:
+            nc.vector.memset(page[:], 0.0)
         nc.gpsimd.memset(w2_sc[:].rearrange("p a n -> p (a n)").bitcast(I32), 0)
         make_identity(nc, ident[:])
 
@@ -121,8 +119,8 @@ def tile_list_opposition_docket_scores_kernel(
 
         def round_w1(engine_copy, grouped, a, b, i0, i1):
             engine_copy(
-                grouped[:].rearrange("p (i m j) -> p m j i", i=i1 - i0, j=4),
-                w1_raw[a, b][:].rearrange("p j (m i) -> p m j i", i=4)[:, :, :, i0:i1],
+                grouped[:].rearrange("p (i m j) -> p i m j", i=i1 - i0, j=4),
+                w1_raw[a, b][:].rearrange("p j (m i) -> p i m j", i=4)[:, i0:i1, :, :],
             )
 
         def quantise_w1(grouped, a, b, i0, i1, first):

@@ -16,11 +16,14 @@ FP8X4 = mybir.dt.float8_e4m3fn_x4
 FP4X4 = mybir.dt.float4_e2m1fn_x4
 ALU = mybir.AluOpType
 COPY = mybir.ActivationFunctionType.Copy
+RELU = mybir.ActivationFunctionType.Relu
 
 P = 128
 HALF = 512
-CHUNKS = (256, 256, 256, 128, 128)
-WEIGHT_SLOTS = ("slot_wg0", "slot_wg1", "slot_wg0", "slot_q", "slot_wg1", "slot_wg0", "slot_q", "z0_1")
+MX_BANKS = 4
+CHUNKS = (128, 256, 256, 256, 128)
+FLOORED_SLOTS = (None, "slot_h1", "slot_h2", "slot_h0", "slot_wg0", "slot_h1", "slot_h2", "slot_h0")
+PICKED_SLOTS = ("least1_0", "least3_1", "least4_1", "least5_1", "least6_1", "least7_0")
 
 
 def tile_list_opposition_docket_scores_kernel(
@@ -51,7 +54,7 @@ def tile_list_opposition_docket_scores_kernel(
         nc.sync.dma_start(list2[:], offs2)
         gain_sb = held([P, 2, 4], F32, "gain_sb")
         nc.sync.dma_start(gain_sb[:], gain.rearrange("(b p i) -> p b i", b=2, i=4))
-        wgs_sb = [held([P, HALF], F32, f"wgs{h}") for h in range(2)]
+        wgs_sb = held([P, S], F32, "wgs_sb")
         tab = [held([P, T], I32, f"tab{a}", f"big{a}") for a in range(2)]
 
         def load_tab(a):
@@ -63,7 +66,7 @@ def tile_list_opposition_docket_scores_kernel(
                 tab_sc[32 * q : 32 * q + 8, :].bitcast(I32), tab_scales[:, 4 * q : 4 * q + 4, :].bitcast(I32)
             )
         for page in pages:
-            nc.vector.memset(page[:], 0.0)
+            nc.vector.memset(page[:].bitcast(I32), 0)
         nc.gpsimd.memset(w2_sc[:].rearrange("p a n -> p (a n)").bitcast(I32), 0)
         make_identity(nc, ident[:])
 
@@ -76,14 +79,8 @@ def tile_list_opposition_docket_scores_kernel(
             least_sb[s, h] = half[:]
 
         def load_least(s):
-            if s <= 4:
-                for h in range(2):
-                    load_least_half(s, h)
-            else:
-                whole = held([P, S], F32, f"least{s}")
-                nc.sync.dma_start(whole[:], least_rows[s // 4, s % 4])
-                for h in range(2):
-                    least_sb[s, h] = whole[:, HALF * h : HALF * (h + 1)]
+            for h in range(2):
+                load_least_half(s, h)
 
         w1_raw = {}
 
@@ -98,15 +95,14 @@ def tile_list_opposition_docket_scores_kernel(
         load_tab(1)
         load_w1(1, 0)
         load_least_half(0, 0)
-        nc.sync.dma_start(wgs_sb[0][:], wgs[:, 0:HALF])
-        nc.sync.dma_start(wgs_sb[1][:], wgs[:, HALF:S])
+        nc.sync.dma_start(wgs_sb[:, 0:HALF], wgs[:, 0:HALF])
+        nc.sync.dma_start(wgs_sb[:, HALF:S], wgs[:, HALF:S])
         load_least_half(0, 1)
         load_least(1)
         nc.sync.dma_start(list3[:], offs3)
         wgt_sb = held([P, M], F32, "wgt_sb")
         nc.sync.dma_start(wgt_sb[:], wgt)
         load_least(2)
-        load_least(3)
 
         v_sc = held([P, S], U8, "v_sc")
         v_words = [held([P, S], U32, f"v_words{a}") for a in range(2)]
@@ -133,7 +129,7 @@ def tile_list_opposition_docket_scores_kernel(
 
         def similarity(s, j0, width):
             b, i = divmod(s, 4)
-            bank = psum.tile([P, width], F32, name="mx_bank", tag="mx_bank", bufs=4)
+            bank = psum.tile([P, width], F32, name="mx_bank", tag="mx_bank", bufs=MX_BANKS)
             cols = slice(j0, j0 + width)
             for a in range(2):
                 nc.tensor.matmul_mx(
@@ -157,10 +153,10 @@ def tile_list_opposition_docket_scores_kernel(
         g10_first = held([P, HALF], BF16, "g10_first")
         round_w1(nc.vector.tensor_copy, g10_first, 1, 0, 0, 1)
         quantise_w1(g10_first, 1, 0, 0, 1, 0)
-        nc.scalar.activation(wg0[:, 0:HALF], wgs_sb[0][:], COPY, scale=row_gain(0))
+        nc.scalar.activation(wg0[:, 0:HALF], wgs_sb[:, 0:HALF], COPY, scale=row_gain(0))
         g10_rest = held([P, 3 * HALF], BF16, "g10_rest", "slot_q")
         round_w1(nc.scalar.copy, g10_rest, 1, 0, 1, 4)
-        nc.scalar.activation(wg0[:, HALF:S], wgs_sb[1][:], COPY, scale=row_gain(0))
+        nc.scalar.activation(wg0[:, HALF:S], wgs_sb[:, HALF:S], COPY, scale=row_gain(0))
         for j0, width, slot in ((0, 256, "slot_h0"), (256, 256, "slot_h2"), (HALF, HALF, "slot_q")):
             if j0 == HALF:
                 quantise_w1(g10_rest, 1, 0, 1, 2, 1)
@@ -178,7 +174,7 @@ def tile_list_opposition_docket_scores_kernel(
 
         load_w1(0, 1)
         load_w1(1, 1)
-        for s in range(4, 8):
+        for s in range(3, 8):
             load_least(s)
         market_sb = [held([P, 4, M], F32, f"market{b}", f"big{b}") for b in range(2)]
         market_rows = market.rearrange("(b p i) m -> b p i m", b=2, i=4)
@@ -194,14 +190,52 @@ def tile_list_opposition_docket_scores_kernel(
 
         floored_of, weight_of, picked0 = {}, {}, {}
 
-        def weigh(s):
-            slot = WEIGHT_SLOTS[s]
+        def weigh(s, slot):
             weight_of[s] = held([P, S], F32, f"wg{s}", slot)
+            nc.scalar.activation(weight_of[s][:], wgs_sb[:], COPY, scale=row_gain(s))
+
+        def add_turned(bank, terms):
+            count = bank.shape[1]
+            for t, term in enumerate(terms):
+                for k in range(count):
+                    nc.tensor.matmul(
+                        bank[:, k, :],
+                        lhsT=term(k),
+                        rhs=ident[:],
+                        is_transpose=True,
+                        start=(t == 0 and k == 0),
+                        stop=(t == len(terms) - 1 and k == count - 1),
+                    )
+
+        def blocks(ap):
+            return lambda k: ap[:, P * k : P * (k + 1)]
+
+        def floor_by_transposes(s):
+            floored_of[s] = held([P, S], F32, f"floored{s}", FLOORED_SLOTS[s])
+            weight_of[s] = wgs_sb
             for h in range(2):
-                nc.scalar.activation(weight_of[s][:, HALF * h : HALF * (h + 1)], wgs_sb[h][:], COPY, scale=row_gain(s))
+                bank = similarity(s, HALF * h, HALF)
+                minus_sim = turn([P, HALF], F32, "minus_sim", 2)
+                nc.scalar.activation(minus_sim[:], bank[:], COPY, scale=-1.0)
+                gap = psum.tile([P, 4, P], F32, name="turned", tag="turned", bufs=2)
+                add_turned(gap, [blocks(least_sb[s, h]), blocks(minus_sim[:])])
+                sim_turned = psum.tile([P, 4, P], F32, name="turned", tag="turned", bufs=2)
+                add_turned(sim_turned, [blocks(minus_sim[:])])
+                lift = turn([P, HALF], F32, "lift", 2)
+                nc.scalar.activation(lift[:], gap[:].rearrange("j k p -> j (k p)"), RELU)
+                base = turn([P, HALF], F32, "base", 2)
+                nc.scalar.activation(base[:], sim_turned[:].rearrange("j k p -> j (k p)"), COPY, scale=-1.0)
+                total = psum.tile([P, 4, P], F32, name="back", tag="back", bufs=2)
+                add_turned(total, [blocks(lift[:]), blocks(base[:])])
+                nc.scalar.activation(
+                    floored_of[s][:, HALF * h : HALF * (h + 1)],
+                    total[:].rearrange("p k j -> p (k j)"),
+                    COPY,
+                    scale=row_gain(s),
+                )
 
         def floor(s):
-            floored_of[s] = held([P, S], F32, f"floored{s}", f"slot_h{s % 3}")
+            floored_of[s] = held([P, S], F32, f"floored{s}", FLOORED_SLOTS[s])
             for h in range(2):
                 cols = slice(HALF * h, HALF * (h + 1))
                 bank = similarity(s, HALF * h, HALF)
@@ -211,62 +245,71 @@ def tile_list_opposition_docket_scores_kernel(
             nc.vector.tensor_tensor(pages[s % 4][:].indirect(list2[:]), floored_of[s][:], weight_of[s][:], ALU.mult)
 
         def pick_whole(s):
-            picked0[s] = held([P, M], F32, f"picked{s}", f"least{s + 1}_0")
-            nc.vector.tensor_tensor(picked0[s][:], pages[s][:].indirect(list3[:]), wgt_sb[:], ALU.mult)
+            picked0[s] = held([P, M], F32, f"picked{s}", PICKED_SLOTS[s])
+            nc.vector.tensor_tensor(picked0[s][:], pages[s % 4][:].indirect(list3[:]), wgt_sb[:], ALU.mult)
 
-        weigh(1)
+        weigh(1, "slot_wg1")
         floor(1)
         pick_whole(0)
         put(1)
-        weigh(2)
-        floor(2)
-        pick_whole(1)
+        floor_by_transposes(2)
         put(2)
         for a, slot in enumerate(("slot_p", "slot_q")):
             grouped = held([P, 4 * HALF], BF16, f"g{a}1", slot)
             round_w1(nc.scalar.copy, grouped, a, 1, 0, 4)
             quantise_w1(grouped, a, 1, 0, 4, 0)
-        weigh(3)
-        floor(3)
-        pick_whole(2)
-        put(3)
-        weigh(4)
-        floor(4)
-        pick_whole(3)
-        for s in range(4, 7):
-            if s < 6:
-                weigh(s + 1)
-            floor(s + 1)
+        for s in range(3, 7):
+            floor_by_transposes(s)
+            pick_whole(s - 2)
             put(s)
+        floor(7)
+        pick_whole(5)
 
-        def interleave(b, mb, picked_block, z_words):
-            cols = slice(P * mb, P * (mb + 1))
-            turned = psum.tile([P, 4, P], F32, name="turned", tag="turned", bufs=2)
-            for i in range(4):
-                nc.tensor.matmul(turned[:, i, :], lhsT=market_sb[b][:, i, cols], rhs=ident[:], is_transpose=True, start=(i == 0), stop=False)
-            for i in range(4):
-                nc.tensor.matmul(turned[:, i, :], lhsT=picked_block(i), rhs=ident[:], is_transpose=True, start=False, stop=(i == 3))
-            pairs = turn([P, 4 * P], BF16, "pairs", 3)
-            nc.scalar.copy(
-                pairs[:].rearrange("m (u p e) -> m u p e", u=2, e=2),
-                turned[:].rearrange("m (u e) p -> m u p e", u=2),
+        def pair_rows(b, u, m0, width, picked_block, pairs):
+            count = width // P
+            turned = psum.tile([P, 2 * count, P], F32, name="turned", tag="turned", bufs=2)
+            add_turned(
+                turned,
+                [
+                    lambda k: market_sb[b][:, 2 * u + k % 2, m0 + P * (k // 2) : m0 + P * (k // 2 + 1)],
+                    lambda k: picked_block(k % 2, k // 2),
+                ],
             )
-            back = psum.tile([P, 2, P], F32, name="back", tag="back", bufs=2)
-            for u in range(2):
-                nc.tensor.transpose(back[:, u, :], pairs[:].bitcast(F32)[:, P * u : P * (u + 1)], ident[:])
-            nc.scalar.copy(z_words.rearrange("p (m u) -> p m u", u=2), back[:].rearrange("p u m -> p m u"))
+            nc.scalar.copy(
+                pairs.rearrange("m (k p e) -> m k p e", k=count, e=2),
+                turned[:].rearrange("m (k e) p -> m k p e", e=2),
+            )
+            return pairs.bitcast(F32)
+
+        def whole_pairs(b, u, m0, width, pairs):
+            return pair_rows(
+                b, u, m0, width, lambda e, k: picked0[4 * b + 2 * u + e][:, m0 + P * k : m0 + P * (k + 1)], pairs
+            )
+
+        def high_pairs(width):
+            return turn([P, 2 * width], BF16, "high_pairs", 2)[:]
+
+        def turn_back(words, z_words):
+            count = words[0].shape[1] // P
+            back = psum.tile([P, count, 2, P], F32, name="back", tag="back", bufs=2)
+            for k in range(count):
+                for u in range(2):
+                    nc.tensor.transpose(back[:, k, u, :], words[u][:, P * k : P * (k + 1)], ident[:])
+            nc.scalar.copy(z_words.rearrange("p (k m u) -> p k m u", k=count, u=2), back[:].rearrange("p k u m -> p k m u"))
 
         z0_codes = held([P, M], U32, "z0_codes")
         z0_sc = held([P, M], U8, "z0_sc")
+        low0_tile = held([P, 2 * M], BF16, "low0", "tab_sc")
+        low0 = [whole_pairs(0, 0, m0, 2 * P, low0_tile[:, 2 * m0 : 2 * m0 + 4 * P]) for m0 in range(0, M, 2 * P)]
         for h in range(2):
             z0 = held([P, 4 * HALF], BF16, f"z0_{h}")
-            for k in range(4):
-                mb = 4 * h + k
-                interleave(0, mb, lambda i: picked0[i][:, P * mb : P * (mb + 1)], z0[:].bitcast(F32)[:, 2 * P * k : 2 * P * (k + 1)])
+            for k in range(2):
+                c = 2 * h + k
+                turn_back([low0[c], whole_pairs(0, 1, 2 * P * c, 2 * P, high_pairs(2 * P))], z0[:].bitcast(F32)[:, HALF * k : HALF * (k + 1)])
             cols = slice(HALF * h, HALF * (h + 1))
             nc.vector.quantize_mx(out=z0_codes[:, cols].bitcast(FP8X4), scales=z0_sc[:, cols], in_=z0[:])
 
-        weigh(7)
+        weigh(7, "z0_0")
         put(7)
 
         cap_rows = cap.rearrange("(nb p) m -> p nb m", p=P)
@@ -275,7 +318,7 @@ def tile_list_opposition_docket_scores_kernel(
             nc.sync.dma_start(cap_sb[h][:], cap_rows[:, :, HALF * h : HALF * (h + 1)])
         out_rows = out.rearrange("(nb p) m -> p nb m", p=P)
 
-        def scores_pass(bank, b, codes, scales):
+        def scores_pass(bank, b, codes, scales, opens):
             for nb in range(4):
                 nc.tensor.matmul_mx(
                     out=bank[:, nb, :],
@@ -283,54 +326,63 @@ def tile_list_opposition_docket_scores_kernel(
                     lhsT_scale=w2_sc[:, b, P * nb : P * (nb + 1)],
                     rhs=codes.bitcast(FP8X4),
                     rhs_scale=scales,
-                    start=(b == 0 and nb == 0),
-                    stop=(b == 1 and nb == 3),
+                    start=(opens and nb == 0),
+                    stop=(not opens and nb == 3),
                 )
 
-        chunk_slots = ("slot_h1", "z0_1", "z1_0", "z1_2", "z1_4")
-        blocks1 = {}
+        starts = [sum(CHUNKS[:c]) for c in range(len(CHUNKS))]
+        low1_tile = held([P, 2 * M], BF16, "low1", "slot_p")
+        low1 = [whole_pairs(1, 0, m0, width, low1_tile[:, 2 * m0 : 2 * (m0 + width)]) for m0, width in zip(starts, CHUNKS)]
+        picked1, open_banks = {}, {}
 
-        def pick_chunk(c):
-            m0, width = sum(CHUNKS[:c]), CHUNKS[c]
-            chunk = held([P, 4, width], F32, f"picked1_{c}", chunk_slots[c])
-            for i in range(4):
-                nc.vector.tensor_tensor(
-                    chunk[:, i, :],
-                    pages[i][:].indirect(list3[:, m0 // 16 : (m0 + width) // 16]),
-                    wgt_sb[:, m0 : m0 + width],
-                    ALU.mult,
-                )
-            for k in range(width // P):
-                blocks1[m0 // P + k] = (chunk, k)
+        def pick_chunks(first, last, slot):
+            base = starts[first]
+            picked = held([P, 2 * sum(CHUNKS[first:last])], F32, f"picked1_{first}", slot)
+            for c in range(first, last):
+                m0, width = starts[c], CHUNKS[c]
+                picked1[c] = picked[:, 2 * (m0 - base) : 2 * (m0 - base + width)].rearrange("p (e m) -> p e m", e=2)
+                for e in range(2):
+                    nc.vector.tensor_tensor(
+                        picked1[c][:, e, :],
+                        pages[2 + e][:].indirect(list3[:, m0 // 16 : (m0 + width) // 16]),
+                        wgt_sb[:, m0 : m0 + width],
+                        ALU.mult,
+                    )
 
-        open_banks = {}
-
-        def second_pass(mb):
-            chunk, k = blocks1[mb]
+        def first_rows(mb, opens):
             cols = slice(P * mb, P * (mb + 1))
-            bank = psum.tile([P, 4, P], F32, name="mx_bank", tag="mx_bank", bufs=4)
-            scores_pass(bank, 0, z0_codes[:, cols], z0_sc[:, cols])
-            z1 = held([P, 4 * P], BF16, f"z1_{mb}")
-            interleave(1, mb, lambda i: chunk[:, i, P * k : P * (k + 1)], z1[:].bitcast(F32))
-            codes = turn([P, P], U32, "z1_codes", 3)
-            scales = turn([P, P], U8, "z1_sc", 3)
+            scores_pass(open_banks[mb], 0, z0_codes[:, cols], z0_sc[:, cols], opens)
+
+        def second_product(c):
+            m0, width = starts[c], CHUNKS[c]
+            for mb in range(m0 // P, (m0 + width) // P):
+                open_banks[mb] = psum.tile([P, 4, P], F32, name="mx_bank", tag="mx_bank", bufs=MX_BANKS)
+                if mb < MX_BANKS:
+                    first_rows(mb, True)
+            high = pair_rows(1, 1, m0, width, lambda e, k: picked1[c][:, e, P * k : P * (k + 1)], high_pairs(width))
+            z1 = held([P, 4 * width], BF16, "z1_0") if c == 0 else turn([P, 4 * width], BF16, "z1", 2)
+            turn_back([low1[c], high], z1[:].bitcast(F32))
+            codes = held([P, width], U32, f"z1_codes{c}")
+            scales = held([P, width], U8, f"z1_sc{c}")
             nc.vector.quantize_mx(out=codes[:].bitcast(FP8X4), scales=scales[:], in_=z1[:])
-            scores_pass(bank, 1, codes[:], scales[:])
-            open_banks[mb] = bank
+            for k in range(width // P):
+                cols = slice(P * k, P * (k + 1))
+                mb = m0 // P + k
+                scores_pass(open_banks[mb], 1, codes[:, cols], scales[:, cols], mb >= MX_BANKS)
+                if mb >= MX_BANKS:
+                    first_rows(mb, False)
 
-        def finish(mb):
-            cols = slice(P * mb, P * (mb + 1))
-            bank = open_banks[mb]
-            result = turn([P, 4, P], F32, "result", 4)
-            nc.vector.tensor_tensor(result[:], bank[:], cap_sb[mb // 4][:, :, P * (mb % 4) : P * (mb % 4 + 1)], ALU.min)
-            nc.sync.dma_start(out_rows[:, :, cols], result[:])
+        def finish(c):
+            for mb in range(starts[c] // P, (starts[c] + CHUNKS[c]) // P):
+                result = turn([P, 4, P], F32, "result", 3)
+                cap_block = cap_sb[mb // 4][:, :, P * (mb % 4) : P * (mb % 4 + 1)]
+                nc.vector.tensor_tensor(result[:], open_banks[mb][:], cap_block, ALU.min)
+                nc.sync.dma_start(out_rows[:, :, P * mb : P * (mb + 1)], result[:])
 
-        pick_chunk(0)
-        pick_chunk(1)
-        for pair in range(4):
-            second_pass(2 * pair)
-            second_pass(2 * pair + 1)
-            if pair + 2 < len(CHUNKS):
-                pick_chunk(pair + 2)
-            finish(2 * pair)
-            finish(2 * pair + 1)
+        pick_chunks(0, 3, "slot_h0")
+        second_product(0)
+        pick_chunks(3, 5, "z1_0")
+        for c in range(1, len(CHUNKS)):
+            finish(c - 1)
+            second_product(c)
+        finish(len(CHUNKS) - 1)

from contextlib import ExitStack

import concourse.mybir as mybir
from concourse.masks import make_identity

K, T, S, T2, M, H, N = 1024, 4096, 1024, 2048, 1024, 1024, 512
FLOPS = 2 * K * H * S + 2 * H * N * M

F32 = mybir.dt.float32
BF16 = mybir.dt.bfloat16
I32 = mybir.dt.int32
U32 = mybir.dt.uint32
U16 = mybir.dt.uint16
U8 = mybir.dt.uint8
FP8X4 = mybir.dt.float8_e4m3fn_x4
FP4X4 = mybir.dt.float4_e2m1fn_x4
ALU = mybir.AluOpType
COPY = mybir.ActivationFunctionType.Copy
RELU = mybir.ActivationFunctionType.Relu

P = 128
HALF = 512
MX_BANKS = 4
CHUNKS = (128, 256, 256, 256, 128)
FLOORED_SLOTS = (None, "slot_h1", "slot_h2", "slot_h0", "slot_wg0", "slot_h1", "slot_h2", "slot_h0")
PICKED_SLOTS = ("least1_0", "least3_1", "least4_1", "least5_1", "least6_1", "least7_0")


def tile_list_opposition_docket_scores_kernel(
    tc, tab_words, tab_scales, offs, offs2, offs3, w1, least, gain, wgs, wgt, market, w2_words, w2_scales, cap, out
):
    nc = tc.nc
    with ExitStack() as ctx:
        keep = ctx.enter_context(tc.tile_pool(name="keep", bufs=1))
        ring = ctx.enter_context(tc.tile_pool(name="ring", bufs=1))
        psum = ctx.enter_context(tc.psum_pool(name="psum", bufs=1))

        def held(shape, dtype, name, tag=None):
            return keep.tile(shape, dtype, name=name, tag=tag or name, align_bytes=64)

        def turn(shape, dtype, tag, bufs):
            return ring.tile(shape, dtype, name=tag, tag=tag, bufs=bufs, align_bytes=64)

        tab_sc = held([P, T], U8, "tab_sc")
        nc.vector.memset(tab_sc[:].bitcast(I32), 0)
        pages = [held([P, T2], F32, f"page{i}") for i in range(4)]
        w2_sc = held([P, 2, N], U8, "w2_sc")
        ident = held([P, P], F32, "ident")

        list1 = held([P, S // 16], U16, "list1")
        list2 = held([P, S // 16], U16, "list2")
        list3 = held([P, M // 16], U16, "list3")
        nc.sync.dma_start(list1[:], offs)
        nc.sync.dma_start(list2[:], offs2)
        gain_sb = held([P, 2, 4], F32, "gain_sb")
        nc.sync.dma_start(gain_sb[:], gain.rearrange("(b p i) -> p b i", b=2, i=4))
        wgs_sb = held([P, S], F32, "wgs_sb")
        tab = [held([P, T], I32, f"tab{a}", f"big{a}") for a in range(2)]

        def load_tab(a):
            nc.sync.dma_start(tab[a][:], tab_words[a].rearrange("p t i -> p (t i)").bitcast(I32))

        load_tab(0)
        for q in range(4):
            nc.scalar.dma_start(
                tab_sc[32 * q : 32 * q + 8, :].bitcast(I32), tab_scales[:, 4 * q : 4 * q + 4, :].bitcast(I32)
            )
        for page in pages:
            nc.vector.memset(page[:].bitcast(I32), 0)
        nc.gpsimd.memset(w2_sc[:].rearrange("p a n -> p (a n)").bitcast(I32), 0)
        make_identity(nc, ident[:])

        least_rows = least.rearrange("(b p i) j -> b i p j", b=2, i=4)
        least_sb = {}

        def load_least_half(s, h):
            half = held([P, HALF], F32, f"least{s}_{h}")
            nc.sync.dma_start(half[:], least_rows[s // 4, s % 4][:, HALF * h : HALF * (h + 1)])
            least_sb[s, h] = half[:]

        def load_least(s):
            for h in range(2):
                load_least_half(s, h)

        w1_raw = {}

        def load_w1(a, b):
            w1_raw[a, b] = held([P, 4, HALF], F32, f"w1_raw{a}{b}", f"w1_raw{a}")
            nc.sync.dma_start(
                w1_raw[a, b][:],
                w1[HALF * a : HALF * (a + 1), HALF * b : HALF * (b + 1)].rearrange("(p j) c -> p j c", j=4),
            )

        load_w1(0, 0)
        load_tab(1)
        load_w1(1, 0)
        load_least_half(0, 0)
        nc.sync.dma_start(wgs_sb[:, 0:HALF], wgs[:, 0:HALF])
        nc.sync.dma_start(wgs_sb[:, HALF:S], wgs[:, HALF:S])
        load_least_half(0, 1)
        load_least(1)
        nc.sync.dma_start(list3[:], offs3)
        wgt_sb = held([P, M], F32, "wgt_sb")
        nc.sync.dma_start(wgt_sb[:], wgt)
        load_least(2)

        v_sc = held([P, S], U8, "v_sc")
        v_words = [held([P, S], U32, f"v_words{a}") for a in range(2)]
        nc.vector.tensor_copy(v_sc[:], tab_sc[:].indirect(list1[:]))
        for a in range(2):
            nc.vector.tensor_copy(v_words[a][:], tab[a][:].bitcast(U32).indirect(list1[:]))

        w1_codes = {(a, b): held([P, HALF], U32, f"w1_codes{a}{b}") for a in range(2) for b in range(2)}
        w1_sc = {(a, b): held([P, HALF], U8, f"w1_sc{a}{b}") for a in range(2) for b in range(2)}

        def round_w1(engine_copy, grouped, a, b, i0, i1):
            engine_copy(
                grouped[:].rearrange("p (i m j) -> p i m j", i=i1 - i0, j=4),
                w1_raw[a, b][:].rearrange("p j (m i) -> p i m j", i=4)[:, i0:i1, :, :],
            )

        def quantise_w1(grouped, a, b, i0, i1, first):
            cols = slice(P * i0, P * i1)
            nc.vector.quantize_mx(
                out=w1_codes[a, b][:, cols].bitcast(FP8X4),
                scales=w1_sc[a, b][:, cols],
                in_=grouped[:, HALF * (i0 - first) : HALF * (i1 - first)],
            )

        def similarity(s, j0, width):
            b, i = divmod(s, 4)
            bank = psum.tile([P, width], F32, name="mx_bank", tag="mx_bank", bufs=MX_BANKS)
            cols = slice(j0, j0 + width)
            for a in range(2):
                nc.tensor.matmul_mx(
                    out=bank[:],
                    lhsT=w1_codes[a, b][:, P * i : P * (i + 1)].bitcast(FP8X4),
                    lhsT_scale=w1_sc[a, b][:, P * i : P * (i + 1)],
                    rhs=v_words[a][:, cols].bitcast(FP8X4),
                    rhs_scale=v_sc[4 * a : P, cols],
                    start=(a == 0),
                    stop=(a == 1),
                )
            return bank

        def row_gain(s):
            return gain_sb[:, s // 4, s % 4 : s % 4 + 1]

        wg0 = held([P, S], F32, "wg0", "slot_wg0")
        g00 = held([P, 4 * HALF], BF16, "g00", "slot_p")
        round_w1(nc.scalar.copy, g00, 0, 0, 0, 4)
        quantise_w1(g00, 0, 0, 0, 4, 0)
        g10_first = held([P, HALF], BF16, "g10_first")
        round_w1(nc.vector.tensor_copy, g10_first, 1, 0, 0, 1)
        quantise_w1(g10_first, 1, 0, 0, 1, 0)
        nc.scalar.activation(wg0[:, 0:HALF], wgs_sb[:, 0:HALF], COPY, scale=row_gain(0))
        g10_rest = held([P, 3 * HALF], BF16, "g10_rest", "slot_q")
        round_w1(nc.scalar.copy, g10_rest, 1, 0, 1, 4)
        nc.scalar.activation(wg0[:, HALF:S], wgs_sb[:, HALF:S], COPY, scale=row_gain(0))
        for j0, width, slot in ((0, 256, "slot_h0"), (256, 256, "slot_h2"), (HALF, HALF, "slot_q")):
            if j0 == HALF:
                quantise_w1(g10_rest, 1, 0, 1, 2, 1)
                quantise_w1(g10_rest, 1, 0, 2, 4, 1)
            bank = similarity(0, j0, width)
            floored = held([P, width], F32, f"floored0_{j0}", slot)
            c0 = j0 % HALF
            nc.vector.tensor_tensor(floored[:], bank[:], least_sb[0, j0 // HALF][:, c0 : c0 + width], ALU.max)
            nc.vector.tensor_tensor(
                pages[0][:].indirect(list2[:, j0 // 16 : (j0 + width) // 16]),
                floored[:],
                wg0[:, j0 : j0 + width],
                ALU.mult,
            )

        load_w1(0, 1)
        load_w1(1, 1)
        for s in range(3, 8):
            load_least(s)
        market_sb = [held([P, 4, M], F32, f"market{b}", f"big{b}") for b in range(2)]
        market_rows = market.rearrange("(b p i) m -> b p i m", b=2, i=4)
        nc.sync.dma_start(market_sb[0][:], market_rows[0])
        w2_sb = held([P, 2, 2 * N], U8, "w2_sb")
        nc.sync.dma_start(w2_sb[:].bitcast(I32), w2_words.rearrange("a p c -> p a c").bitcast(I32))
        for q in range(4):
            nc.sync.dma_start(
                w2_sc[32 * q : 32 * q + 4, :, :].bitcast(I32),
                w2_scales[:, 4 * q : 4 * q + 4, :].rearrange("a r n -> r a n").bitcast(I32),
            )
        nc.sync.dma_start(market_sb[1][:], market_rows[1])

        floored_of, weight_of, picked0 = {}, {}, {}

        def weigh(s, slot):
            weight_of[s] = held([P, S], F32, f"wg{s}", slot)
            nc.scalar.activation(weight_of[s][:], wgs_sb[:], COPY, scale=row_gain(s))

        def add_turned(bank, terms):
            count = bank.shape[1]
            for t, term in enumerate(terms):
                for k in range(count):
                    nc.tensor.matmul(
                        bank[:, k, :],
                        lhsT=term(k),
                        rhs=ident[:],
                        is_transpose=True,
                        start=(t == 0 and k == 0),
                        stop=(t == len(terms) - 1 and k == count - 1),
                    )

        def blocks(ap):
            return lambda k: ap[:, P * k : P * (k + 1)]

        def floor_by_transposes(s):
            floored_of[s] = held([P, S], F32, f"floored{s}", FLOORED_SLOTS[s])
            weight_of[s] = wgs_sb
            for h in range(2):
                bank = similarity(s, HALF * h, HALF)
                minus_sim = turn([P, HALF], F32, "minus_sim", 2)
                nc.scalar.activation(minus_sim[:], bank[:], COPY, scale=-1.0)
                gap = psum.tile([P, 4, P], F32, name="turned", tag="turned", bufs=2)
                add_turned(gap, [blocks(least_sb[s, h]), blocks(minus_sim[:])])
                sim_turned = psum.tile([P, 4, P], F32, name="turned", tag="turned", bufs=2)
                add_turned(sim_turned, [blocks(minus_sim[:])])
                lift = turn([P, HALF], F32, "lift", 2)
                nc.scalar.activation(lift[:], gap[:].rearrange("j k p -> j (k p)"), RELU)
                base = turn([P, HALF], F32, "base", 2)
                nc.scalar.activation(base[:], sim_turned[:].rearrange("j k p -> j (k p)"), COPY, scale=-1.0)
                total = psum.tile([P, 4, P], F32, name="back", tag="back", bufs=2)
                add_turned(total, [blocks(lift[:]), blocks(base[:])])
                nc.scalar.activation(
                    floored_of[s][:, HALF * h : HALF * (h + 1)],
                    total[:].rearrange("p k j -> p (k j)"),
                    COPY,
                    scale=row_gain(s),
                )

        def floor(s):
            floored_of[s] = held([P, S], F32, f"floored{s}", FLOORED_SLOTS[s])
            for h in range(2):
                cols = slice(HALF * h, HALF * (h + 1))
                bank = similarity(s, HALF * h, HALF)
                nc.vector.tensor_tensor(floored_of[s][:, cols], bank[:], least_sb[s, h], ALU.max)

        def put(s):
            nc.vector.tensor_tensor(pages[s % 4][:].indirect(list2[:]), floored_of[s][:], weight_of[s][:], ALU.mult)

        def pick_whole(s):
            picked0[s] = held([P, M], F32, f"picked{s}", PICKED_SLOTS[s])
            nc.vector.tensor_tensor(picked0[s][:], pages[s % 4][:].indirect(list3[:]), wgt_sb[:], ALU.mult)

        weigh(1, "slot_wg1")
        floor(1)
        pick_whole(0)
        put(1)
        floor_by_transposes(2)
        put(2)
        for a, slot in enumerate(("slot_p", "slot_q")):
            grouped = held([P, 4 * HALF], BF16, f"g{a}1", slot)
            round_w1(nc.scalar.copy, grouped, a, 1, 0, 4)
            quantise_w1(grouped, a, 1, 0, 4, 0)
        for s in range(3, 7):
            floor_by_transposes(s)
            pick_whole(s - 2)
            put(s)
        floor(7)
        pick_whole(5)

        def pair_rows(b, u, m0, width, picked_block, pairs):
            count = width // P
            turned = psum.tile([P, 2 * count, P], F32, name="turned", tag="turned", bufs=2)
            add_turned(
                turned,
                [
                    lambda k: market_sb[b][:, 2 * u + k % 2, m0 + P * (k // 2) : m0 + P * (k // 2 + 1)],
                    lambda k: picked_block(k % 2, k // 2),
                ],
            )
            nc.scalar.copy(
                pairs.rearrange("m (k p e) -> m k p e", k=count, e=2),
                turned[:].rearrange("m (k e) p -> m k p e", e=2),
            )
            return pairs.bitcast(F32)

        def whole_pairs(b, u, m0, width, pairs):
            return pair_rows(
                b, u, m0, width, lambda e, k: picked0[4 * b + 2 * u + e][:, m0 + P * k : m0 + P * (k + 1)], pairs
            )

        def high_pairs(width):
            return turn([P, 2 * width], BF16, "high_pairs", 2)[:]

        def turn_back(words, z_words):
            count = words[0].shape[1] // P
            back = psum.tile([P, count, 2, P], F32, name="back", tag="back", bufs=2)
            for k in range(count):
                for u in range(2):
                    nc.tensor.transpose(back[:, k, u, :], words[u][:, P * k : P * (k + 1)], ident[:])
            nc.scalar.copy(z_words.rearrange("p (k m u) -> p k m u", k=count, u=2), back[:].rearrange("p k u m -> p k m u"))

        z0_codes = held([P, M], U32, "z0_codes")
        z0_sc = held([P, M], U8, "z0_sc")
        low0_tile = held([P, 2 * M], BF16, "low0", "tab_sc")
        low0 = [whole_pairs(0, 0, m0, 2 * P, low0_tile[:, 2 * m0 : 2 * m0 + 4 * P]) for m0 in range(0, M, 2 * P)]
        for h in range(2):
            z0 = held([P, 4 * HALF], BF16, f"z0_{h}")
            for k in range(2):
                c = 2 * h + k
                turn_back([low0[c], whole_pairs(0, 1, 2 * P * c, 2 * P, high_pairs(2 * P))], z0[:].bitcast(F32)[:, HALF * k : HALF * (k + 1)])
            cols = slice(HALF * h, HALF * (h + 1))
            nc.vector.quantize_mx(out=z0_codes[:, cols].bitcast(FP8X4), scales=z0_sc[:, cols], in_=z0[:])

        weigh(7, "z0_0")
        put(7)

        cap_rows = cap.rearrange("(nb p) m -> p nb m", p=P)
        cap_sb = [held([P, 4, HALF], F32, f"cap{h}", f"w1_raw{h}") for h in range(2)]
        for h in range(2):
            nc.sync.dma_start(cap_sb[h][:], cap_rows[:, :, HALF * h : HALF * (h + 1)])
        out_rows = out.rearrange("(nb p) m -> p nb m", p=P)

        def scores_pass(bank, b, codes, scales, opens):
            for nb in range(4):
                nc.tensor.matmul_mx(
                    out=bank[:, nb, :],
                    lhsT=w2_sb[:, b, 2 * P * nb : 2 * P * (nb + 1)].bitcast(FP4X4),
                    lhsT_scale=w2_sc[:, b, P * nb : P * (nb + 1)],
                    rhs=codes.bitcast(FP8X4),
                    rhs_scale=scales,
                    start=(opens and nb == 0),
                    stop=(not opens and nb == 3),
                )

        starts = [sum(CHUNKS[:c]) for c in range(len(CHUNKS))]
        low1_tile = held([P, 2 * M], BF16, "low1", "slot_p")
        low1 = [whole_pairs(1, 0, m0, width, low1_tile[:, 2 * m0 : 2 * (m0 + width)]) for m0, width in zip(starts, CHUNKS)]
        picked1, open_banks = {}, {}

        def pick_chunks(first, last, slot):
            base = starts[first]
            picked = held([P, 2 * sum(CHUNKS[first:last])], F32, f"picked1_{first}", slot)
            for c in range(first, last):
                m0, width = starts[c], CHUNKS[c]
                picked1[c] = picked[:, 2 * (m0 - base) : 2 * (m0 - base + width)].rearrange("p (e m) -> p e m", e=2)
                for e in range(2):
                    nc.vector.tensor_tensor(
                        picked1[c][:, e, :],
                        pages[2 + e][:].indirect(list3[:, m0 // 16 : (m0 + width) // 16]),
                        wgt_sb[:, m0 : m0 + width],
                        ALU.mult,
                    )

        def first_rows(mb, opens):
            cols = slice(P * mb, P * (mb + 1))
            scores_pass(open_banks[mb], 0, z0_codes[:, cols], z0_sc[:, cols], opens)

        def second_product(c):
            m0, width = starts[c], CHUNKS[c]
            for mb in range(m0 // P, (m0 + width) // P):
                open_banks[mb] = psum.tile([P, 4, P], F32, name="mx_bank", tag="mx_bank", bufs=MX_BANKS)
                if mb < MX_BANKS:
                    first_rows(mb, True)
            high = pair_rows(1, 1, m0, width, lambda e, k: picked1[c][:, e, P * k : P * (k + 1)], high_pairs(width))
            z1 = held([P, 4 * width], BF16, "z1_0") if c == 0 else turn([P, 4 * width], BF16, "z1", 2)
            turn_back([low1[c], high], z1[:].bitcast(F32))
            codes = held([P, width], U32, f"z1_codes{c}")
            scales = held([P, width], U8, f"z1_sc{c}")
            nc.vector.quantize_mx(out=codes[:].bitcast(FP8X4), scales=scales[:], in_=z1[:])
            for k in range(width // P):
                cols = slice(P * k, P * (k + 1))
                mb = m0 // P + k
                scores_pass(open_banks[mb], 1, codes[:, cols], scales[:, cols], mb >= MX_BANKS)
                if mb >= MX_BANKS:
                    first_rows(mb, False)

        def finish(c):
            for mb in range(starts[c] // P, (starts[c] + CHUNKS[c]) // P):
                result = turn([P, 4, P], F32, "result", 3)
                cap_block = cap_sb[mb // 4][:, :, P * (mb % 4) : P * (mb % 4 + 1)]
                nc.vector.tensor_tensor(result[:], open_banks[mb][:], cap_block, ALU.min)
                nc.sync.dma_start(out_rows[:, :, P * mb : P * (mb + 1)], result[:])

        pick_chunks(0, 3, "slot_h0")
        second_product(0)
        pick_chunks(3, 5, "z1_0")
        for c in range(1, len(CHUNKS)):
            finish(c - 1)
            second_product(c)
        finish(len(CHUNKS) - 1)
